import numpy as np
import ml_dtypes


def mxq(x, axis, fmt="e4m3"):
    dtype, down = {"e4m3": (ml_dtypes.float8_e4m3fn, 7), "e5m2": (ml_dtypes.float8_e5m2, 14)}[fmt]
    v = np.moveaxis(np.asarray(x, np.float32).astype(ml_dtypes.bfloat16).astype(np.float64), axis, -1)
    blocks = v.reshape(v.shape[:-1] + (-1, 32))
    amax = np.abs(blocks).max(-1, keepdims=True)
    byte = np.maximum(np.where(amax > 0, np.frexp(amax)[1] - 1 + 127, 0) - down, 1)
    scale = np.exp2(byte - 127.0)
    codes = (blocks / scale).astype(np.float32).astype(dtype).astype(np.float64)
    return np.moveaxis((codes * scale).reshape(v.shape), -1, axis)


WIDE = False


def mx_kscale(k):
    if not WIDE:
        return np.ones(k)
    levels = np.array([10, -10, 5, -5, 0])
    if k % 512:
        return np.exp2(np.random.permutation(np.resize(levels, k // 32))).repeat(32)
    a = np.empty((k // 512, 16))
    for p in range(k // 512):
        a[p, :8] = np.random.permutation(np.resize(levels, 8))
        for g in range(8):
            far = levels[np.abs(levels - a[p, g]) >= 10]
            a[p, g + 8] = far[np.random.randint(len(far))]
    return np.exp2(a.ravel()).repeat(32)


def f64(x):
    return np.asarray(x).astype(np.float64)


def striped(idx):
    return np.tile(idx.reshape(-1, 16).T, (8, 1)).astype(np.uint16)


def unstriped(offs):
    return offs[:16].T.reshape(-1).astype(np.int64)


def pack_weight(w):
    k, n = w.shape
    w = f64(np.asarray(w, np.float32).astype(ml_dtypes.bfloat16)).reshape(k // 32, 32, n)
    amax = np.abs(w).max(1)
    byte = np.clip(np.where(amax > 0, np.frexp(amax)[1] - 1 + 127 - 7, 1), 1, 254)
    scaled = (w * np.exp2(127.0 - byte)[:, None, :]).reshape(k, n).astype(np.float32)
    words = np.ascontiguousarray(scaled.reshape(k // 512, 128, 4, n).transpose(0, 1, 3, 2)).astype(ml_dtypes.float8_e4m3fn).view(np.uint8)
    return words, np.ascontiguousarray(byte.astype(np.uint8).reshape(k // 512, 16, n))


def unpack_weight(words, scales):
    g, p, n, _ = words.shape
    vals = np.ascontiguousarray(words).view(ml_dtypes.float8_e4m3fn).astype(np.float64) * np.repeat(np.exp2(scales.astype(np.float64) - 127.0), 8, axis=1)[..., None]
    return vals.transpose(0, 1, 3, 2).reshape(g * 512, n)


K, T, E, C, N = 3072, 768, 2, 256, 384


def by_expert(wq, xq):
    return np.concatenate([wq[e].T @ xq[:, e * C:(e + 1) * C] for e in range(E)], axis=1)


def setup_inputs():
    n = np.random.standard_normal
    s = mx_kscale(K)[:, None]
    packed = [pack_weight(m) for m in n((E, K, N)) / np.sqrt(K) / s[None]]
    return {
        "xT": (n((K, T)) * s).astype(np.float32),
        "w_words": np.stack([m[0] for m in packed]),
        "w_scales": np.stack([m[1] for m in packed]),
        "gate": np.tile(np.random.uniform(0.2, 1.0, E * C), (N, 1)).astype(np.float32),
        "offs": striped(np.random.permutation(T)[:E * C]),
    }


def reference(xT, w_words, w_scales, gate, offs):
    idx = unstriped(offs)
    xq = mxq(f64(xT)[:, idx], 0, "e4m3")
    w = np.stack([unpack_weight(w_words[e], w_scales[e]) for e in range(E)])
    y = by_expert(w, xq)
    out = np.zeros((N, T))
    out[:, idx] = f64(gate) * y
    return out

@@ -1,0 +1,116 @@
+from contextlib import ExitStack
+
+import concourse.mybir as mybir
+
+F32 = mybir.dt.float32
+BF16 = mybir.dt.bfloat16
+I32 = mybir.dt.int32
+U32 = mybir.dt.uint32
+U16 = mybir.dt.uint16
+U8 = mybir.dt.uint8
+FP8X4 = mybir.dt.float8_e4m3fn_x4
+MULT = mybir.AluOpType.mult
+
+K, T, E, C, N = 3072, 768, 2, 256, 384
+P = 128
+PASSES = K // 512
+BLOCKS = N // P
+SLOTS = E * C
+FLOPS = 2 * K * N * SLOTS
+
+WIDE = 512
+PLANES = 4
+
+
+def tile_routed_moe_kernel(tc, xT, w_words, w_scales, gate, offs, out):
+    nc = tc.nc
+    with ExitStack() as ctx:
+        held = ctx.enter_context(tc.tile_pool(name="held", bufs=1))
+        psum = ctx.enter_context(tc.psum_pool(name="psum", bufs=1))
+
+        offsets = held.tile([P, SLOTS // 16], U16, name="offsets")
+        raw = [held.tile([P, 4, T], F32, name=f"raw{a}") for a in range(PASSES)]
+        first = [held.tile([P, WIDE, 4], BF16, name=f"first{a}", align_bytes=64) for a in range(PASSES)]
+        second = [held.tile([P, T - WIDE, 4], BF16, name=f"second{a}", align_bytes=64) for a in range(PASSES)]
+        words = [held.tile([P, T], U32, name=f"words{a}", align_bytes=64) for a in range(PASSES)]
+        planes = [held.tile([P, T], U8, name=f"planes{g}", align_bytes=64) for g in range(2)]
+        slot_words = [held.tile([P, SLOTS], U32, name=f"slot_words{a}", align_bytes=64) for a in range(PASSES)]
+        slot_planes = [held.tile([P, SLOTS], U8, name=f"slot_planes{g}", align_bytes=64) for g in range(2)]
+        weights = [held.tile([P, E, N], I32, name=f"weights{a}", align_bytes=64) for a in range(PASSES)]
+        weight_planes = held.tile([P, E * PASSES * N], U8, name="weight_planes", align_bytes=64)
+        gates = held.tile([P, SLOTS], F32, name="gates")
+        windows = [held.tile([P, T], F32, name=f"window{b}") for b in range(BLOCKS)]
+        scaled = [[held.tile([P, C], F32, name=f"scaled{b}_{e}") for e in range(E)] for b in range(BLOCKS)]
+        sums = [[psum.tile([P, C], F32, name=f"sums{b}_{e}") for e in range(E)] for b in range(BLOCKS)]
+
+        nc.vector.memset(weight_planes[:].bitcast(I32), 0)
+        for g in range(2):
+            nc.gpsimd.memset(planes[g][:], 0)
+        for b in range(BLOCKS):
+            nc.gpsimd.memset(windows[b][:], 0.0)
+
+        x_rows = xT.rearrange("(a p t) n -> a p t n", p=P, t=4)
+        w_rows = w_words.rearrange("e a p n r -> e a p (n r)").bitcast(I32).rearrange("e a p n -> a p e n")
+        s_rows = w_scales.bitcast(I32).rearrange("e a q n -> q (e a) n")
+        s_tile = weight_planes[:].bitcast(I32).rearrange("p (s n) -> p s n", s=E * PASSES)
+        for a in range(PASSES):
+            if a in (0, PASSES - 1):
+                nc.sync.dma_start(out=raw[a][:, :, 0:WIDE], in_=x_rows[a][:, :, 0:WIDE])
+                nc.sync.dma_start(out=raw[a][:, :, WIDE:T], in_=x_rows[a][:, :, WIDE:T])
+            else:
+                nc.sync.dma_start(out=raw[a][:], in_=x_rows[a])
+            if a == 0:
+                nc.sync.dma_start(offsets[:], offs)
+                for q in range(4):
+                    nc.sync.dma_start(out=s_tile[32 * q : 32 * q + 4], in_=s_rows[4 * q : 4 * q + 4])
+        for a in range(PASSES):
+            nc.sync.dma_start(out=weights[a][:], in_=w_rows[a])
+            if a == 2:
+                nc.sync.dma_start(out=gates[:], in_=gate[0:P, :])
+
+        def interleave(copy, dst, a, lo, hi, base):
+            copy(
+                out=dst[a][:, lo - base : hi - base, :].rearrange("p (c i) t -> p c t i", i=4),
+                in_=raw[a][:, :, lo:hi].rearrange("p t (c i) -> p c t i", i=4),
+            )
+
+        for a in range(PASSES):
+            g, j = a // PLANES, a % PLANES
+            cut = WIDE if a < PASSES - 1 else 256
+            interleave(nc.scalar.copy, first, a, 0, cut, 0)
+            if cut < WIDE:
+                interleave(nc.vector.tensor_copy, first, a, cut, WIDE, 0)
+            interleave(nc.vector.tensor_copy, second, a, WIDE, T, WIDE)
+            for src, lo, hi in ((first, 0, WIDE), (second, WIDE, T)):
+                nc.vector.quantize_mx(
+                    out=words[a][:, lo:hi].bitcast(FP8X4),
+                    scales=planes[g][4 * j : P, lo:hi],
+                    in_=src[a][:].rearrange("p c t -> p (c t)"),
+                )
+            nc.vector.tensor_copy(out=slot_words[a][:], in_=words[a][:].indirect(offsets[:]))
+            if a in (PLANES - 1, PASSES - 1):
+                nc.vector.tensor_copy(out=slot_planes[g][:], in_=planes[g][:].indirect(offsets[:]))
+
+        for a in range(PASSES):
+            g, j = a // PLANES, a % PLANES
+            for b in range(BLOCKS):
+                for e in range(E):
+                    col = (e * PASSES + a) * N + b * P
+                    nc.tensor.matmul_mx(
+                        out=sums[b][e][:],
+                        lhsT=weights[a][:, e, b * P : (b + 1) * P].bitcast(FP8X4),
+                        lhsT_scale=weight_planes[:, col : col + P],
+                        rhs=slot_words[a][:, e * C : (e + 1) * C].bitcast(FP8X4),
+                        rhs_scale=slot_planes[g][4 * j : P, e * C : (e + 1) * C],
+                        start=(a == 0),
+                        stop=(a == PASSES - 1),
+                    )
+
+        for b in range(BLOCKS):
+            for e in range(E):
+                nc.vector.tensor_tensor(scaled[b][e][:], sums[b][e][:], gates[:, e * C : (e + 1) * C], MULT)
+                nc.vector.tensor_copy(
+                    out=windows[b][:].indirect(offsets[:, e * C // 16 : (e + 1) * C // 16]),
+                    in_=scaled[b][e][:],
+                )
+            nc.sync.dma_start(out=out[b * P : (b + 1) * P, :], in_=windows[b][:])

@@ -36,12 +36,11 @@ def tile_routed_moe_kernel(tc, xT, w_words, w_scales, gate, offs, out):
         planes = [held.tile([P, T], U8, name=f"planes{g}", align_bytes=64) for g in range(2)]
         slot_words = [held.tile([P, SLOTS], U32, name=f"slot_words{a}", align_bytes=64) for a in range(PASSES)]
         slot_planes = [held.tile([P, SLOTS], U8, name=f"slot_planes{g}", align_bytes=64) for g in range(2)]
-        weights = [held.tile([P, E, N], I32, name=f"weights{a}", align_bytes=64) for a in range(PASSES)]
+        weights = [held.tile([P, PASSES, N], I32, name=f"weights{e}", align_bytes=64) for e in range(E)]
         weight_planes = held.tile([P, E * PASSES * N], U8, name="weight_planes", align_bytes=64)
         gates = held.tile([P, SLOTS], F32, name="gates")
         windows = [held.tile([P, T], F32, name=f"window{b}") for b in range(BLOCKS)]
         scaled = [[held.tile([P, C], F32, name=f"scaled{b}_{e}") for e in range(E)] for b in range(BLOCKS)]
-        sums = [[psum.tile([P, C], F32, name=f"sums{b}_{e}") for e in range(E)] for b in range(BLOCKS)]
 
         nc.vector.memset(weight_planes[:].bitcast(I32), 0)
         for g in range(2):
@@ -50,7 +49,7 @@ def tile_routed_moe_kernel(tc, xT, w_words, w_scales, gate, offs, out):
             nc.gpsimd.memset(windows[b][:], 0.0)
 
         x_rows = xT.rearrange("(a p t) n -> a p t n", p=P, t=4)
-        w_rows = w_words.rearrange("e a p n r -> e a p (n r)").bitcast(I32).rearrange("e a p n -> a p e n")
+        w_rows = w_words.rearrange("e a p n r -> e a p (n r)").bitcast(I32).rearrange("e a p n -> e p a n")
         s_rows = w_scales.bitcast(I32).rearrange("e a q n -> q (e a) n")
         s_tile = weight_planes[:].bitcast(I32).rearrange("p (s n) -> p s n", s=E * PASSES)
         for a in range(PASSES):
@@ -63,9 +62,10 @@ def tile_routed_moe_kernel(tc, xT, w_words, w_scales, gate, offs, out):
                 nc.sync.dma_start(offsets[:], offs)
                 for q in range(4):
                     nc.sync.dma_start(out=s_tile[32 * q : 32 * q + 4], in_=s_rows[4 * q : 4 * q + 4])
-        for a in range(PASSES):
-            nc.sync.dma_start(out=weights[a][:], in_=w_rows[a])
-            if a == 2:
+        for e in range(E):
+            for lo, hi in ((0, PLANES), (PLANES, PASSES)):
+                nc.sync.dma_start(out=weights[e][:, lo:hi, :], in_=w_rows[e][:, lo:hi, :])
+            if e == 0:
                 nc.sync.dma_start(out=gates[:], in_=gate[0:P, :])
 
         def interleave(copy, dst, a, lo, hi, base):
@@ -76,12 +76,15 @@ def tile_routed_moe_kernel(tc, xT, w_words, w_scales, gate, offs, out):
 
         for a in range(PASSES):
             g, j = a // PLANES, a % PLANES
-            cut = WIDE if a < PASSES - 1 else 256
-            interleave(nc.scalar.copy, first, a, 0, cut, 0)
-            if cut < WIDE:
-                interleave(nc.vector.tensor_copy, first, a, cut, WIDE, 0)
-            interleave(nc.vector.tensor_copy, second, a, WIDE, T, WIDE)
-            for src, lo, hi in ((first, 0, WIDE), (second, WIDE, T)):
+            if a < PASSES - 1:
+                interleave(nc.scalar.copy, second, a, WIDE, WIDE + 64, WIDE)
+                interleave(nc.vector.tensor_copy, second, a, WIDE + 64, T, WIDE)
+                interleave(nc.scalar.copy, first, a, 0, WIDE, 0)
+            else:
+                interleave(nc.scalar.copy, first, a, 0, 384, 0)
+                interleave(nc.vector.tensor_copy, first, a, 384, WIDE, 0)
+                interleave(nc.vector.tensor_copy, second, a, WIDE, T, WIDE)
+            for src, lo, hi in ((second, WIDE, T), (first, 0, WIDE)):
                 nc.vector.quantize_mx(
                     out=words[a][:, lo:hi].bitcast(FP8X4),
                     scales=planes[g][4 * j : P, lo:hi],
@@ -91,26 +94,34 @@ def tile_routed_moe_kernel(tc, xT, w_words, w_scales, gate, offs, out):
             if a in (PLANES - 1, PASSES - 1):
                 nc.vector.tensor_copy(out=slot_planes[g][:], in_=planes[g][:].indirect(offsets[:]))
 
-        for a in range(PASSES):
+        def multiply(sums, e, b, a):
             g, j = a // PLANES, a % PLANES
-            for b in range(BLOCKS):
-                for e in range(E):
-                    col = (e * PASSES + a) * N + b * P
-                    nc.tensor.matmul_mx(
-                        out=sums[b][e][:],
-                        lhsT=weights[a][:, e, b * P : (b + 1) * P].bitcast(FP8X4),
-                        lhsT_scale=weight_planes[:, col : col + P],
-                        rhs=slot_words[a][:, e * C : (e + 1) * C].bitcast(FP8X4),
-                        rhs_scale=slot_planes[g][4 * j : P, e * C : (e + 1) * C],
-                        start=(a == 0),
-                        stop=(a == PASSES - 1),
-                    )
+            col = (e * PASSES + a) * N + b * P
+            nc.tensor.matmul_mx(
+                out=sums[b][:],
+                lhsT=weights[e][:, a, b * P : (b + 1) * P].bitcast(FP8X4),
+                lhsT_scale=weight_planes[:, col : col + P],
+                rhs=slot_words[a][:, e * C : (e + 1) * C].bitcast(FP8X4),
+                rhs_scale=slot_planes[g][4 * j : P, e * C : (e + 1) * C],
+                start=(a == 0),
+                stop=(a == PASSES - 1),
+            )
 
-        for b in range(BLOCKS):
-            for e in range(E):
-                nc.vector.tensor_tensor(scaled[b][e][:], sums[b][e][:], gates[:, e * C : (e + 1) * C], MULT)
-                nc.vector.tensor_copy(
-                    out=windows[b][:].indirect(offsets[:, e * C // 16 : (e + 1) * C // 16]),
-                    in_=scaled[b][e][:],
+        for e in range(E):
+            sums = [psum.tile([P, C], F32, name=f"sums{b}") for b in range(BLOCKS)]
+            if e == 0:
+                for a in range(PLANES):
+                    for b in range(BLOCKS):
+                        multiply(sums, e, b, a)
+            for b in range(BLOCKS):
+                for a in range(PLANES if e == 0 else 0, PASSES):
+                    multiply(sums, e, b, a)
+                nc.scalar.copy(scaled[b][e][:], sums[b][:])
+                nc.vector.tensor_tensor(
+                    windows[b][:].indirect(offsets[:, e * C // 16 : (e + 1) * C // 16]),
+                    scaled[b][e][:],
+                    gates[:, e * C : (e + 1) * C],
+                    MULT,
                 )
-            nc.sync.dma_start(out=out[b * P : (b + 1) * P, :], in_=windows[b][:])
+                if e == E - 1:
+                    nc.sync.dma_start(out=out[b * P : (b + 1) * P, :], in_=windows[b][:])

@@ -19,6 +19,8 @@ SLOTS = E * C
 FLOPS = 2 * K * N * SLOTS
 
 WIDE = 512
+LOADS = [((0, 512), (512, T)), ((0, 512), (512, T)), ((0, 512), (512, T)), ((0, 512), (512, T)), ((0, 256), (256, 512), (512, T)), ((0, 512), (512, T))]
+ON_SCALAR = [512,512,512,512,640,640]
 PLANES = 4
 
 
@@ -30,8 +32,7 @@ def tile_routed_moe_kernel(tc, xT, w_words, w_scales, gate, offs, out):
 
         offsets = held.tile([P, SLOTS // 16], U16, name="offsets")
         raw = [held.tile([P, 4, T], F32, name=f"raw{a}") for a in range(PASSES)]
-        first = [held.tile([P, WIDE, 4], BF16, name=f"first{a}", align_bytes=64) for a in range(PASSES)]
-        second = [held.tile([P, T - WIDE, 4], BF16, name=f"second{a}", align_bytes=64) for a in range(PASSES)]
+        grouped = [held.tile([P, T, 4], BF16, name=f"grouped{a}", align_bytes=64) for a in range(PASSES)]
         words = [held.tile([P, T], U32, name=f"words{a}", align_bytes=64) for a in range(PASSES)]
         planes = [held.tile([P, T], U8, name=f"planes{g}", align_bytes=64) for g in range(2)]
         slot_words = [held.tile([P, SLOTS], U32, name=f"slot_words{a}", align_bytes=64) for a in range(PASSES)]
@@ -53,11 +54,8 @@ def tile_routed_moe_kernel(tc, xT, w_words, w_scales, gate, offs, out):
         s_rows = w_scales.bitcast(I32).rearrange("e a q n -> q (e a) n")
         s_tile = weight_planes[:].bitcast(I32).rearrange("p (s n) -> p s n", s=E * PASSES)
         for a in range(PASSES):
-            if a in (0, PASSES - 1):
-                nc.sync.dma_start(out=raw[a][:, :, 0:WIDE], in_=x_rows[a][:, :, 0:WIDE])
-                nc.sync.dma_start(out=raw[a][:, :, WIDE:T], in_=x_rows[a][:, :, WIDE:T])
-            else:
-                nc.sync.dma_start(out=raw[a][:], in_=x_rows[a])
+            for lo, hi in LOADS[a]:
+                nc.sync.dma_start(out=raw[a][:, :, lo:hi], in_=x_rows[a][:, :, lo:hi])
             if a == 0:
                 nc.sync.dma_start(offsets[:], offs)
                 for q in range(4):
@@ -68,31 +66,33 @@ def tile_routed_moe_kernel(tc, xT, w_words, w_scales, gate, offs, out):
             if e == 0:
                 nc.sync.dma_start(out=gates[:], in_=gate[0:P, :])
 
-        def interleave(copy, dst, a, lo, hi, base):
+        def interleave(copy, a, lo, hi):
             copy(
-                out=dst[a][:, lo - base : hi - base, :].rearrange("p (c i) t -> p c t i", i=4),
+                out=grouped[a][:, lo:hi, :].rearrange("p (c i) t -> p c t i", i=4),
                 in_=raw[a][:, :, lo:hi].rearrange("p t (c i) -> p c t i", i=4),
             )
 
+        def gather(dst, src, lo, hi):
+            nc.vector.tensor_copy(out=dst[:, lo:hi], in_=src[:].indirect(offsets[:, lo // 16 : hi // 16]))
+
         for a in range(PASSES):
             g, j = a // PLANES, a % PLANES
-            if a < PASSES - 1:
-                interleave(nc.scalar.copy, second, a, WIDE, WIDE + 64, WIDE)
-                interleave(nc.vector.tensor_copy, second, a, WIDE + 64, T, WIDE)
-                interleave(nc.scalar.copy, first, a, 0, WIDE, 0)
-            else:
-                interleave(nc.scalar.copy, first, a, 0, 384, 0)
-                interleave(nc.vector.tensor_copy, first, a, 384, WIDE, 0)
-                interleave(nc.vector.tensor_copy, second, a, WIDE, T, WIDE)
-            for src, lo, hi in ((second, WIDE, T), (first, 0, WIDE)):
+            cut = ON_SCALAR[a]
+            for lo, hi in LOADS[a]:
+                if lo < cut:
+                    interleave(nc.scalar.copy, a, lo, min(hi, cut))
+                if hi > cut:
+                    interleave(nc.vector.tensor_copy, a, max(lo, cut), hi)
+            for lo, hi in ((0, WIDE), (WIDE, T)):
                 nc.vector.quantize_mx(
                     out=words[a][:, lo:hi].bitcast(FP8X4),
                     scales=planes[g][4 * j : P, lo:hi],
-                    in_=src[a][:].rearrange("p c t -> p (c t)"),
+                    in_=grouped[a][:, lo:hi, :].rearrange("p c t -> p (c t)"),
                 )
-            nc.vector.tensor_copy(out=slot_words[a][:], in_=words[a][:].indirect(offsets[:]))
-            if a in (PLANES - 1, PASSES - 1):
-                nc.vector.tensor_copy(out=slot_planes[g][:], in_=planes[g][:].indirect(offsets[:]))
+            for lo, hi in ((0, C), (C, SLOTS)) if a == PASSES - 1 else ((0, SLOTS),):
+                gather(slot_words[a], words[a], lo, hi)
+                if a in (PLANES - 1, PASSES - 1):
+                    gather(slot_planes[g], planes[g], lo, hi)
 
         def multiply(sums, e, b, a):
             g, j = a // PLANES, a % PLANES

@@ -19,8 +19,7 @@ SLOTS = E * C
 FLOPS = 2 * K * N * SLOTS
 
 WIDE = 512
-LOADS = [((0, 512), (512, T)), ((0, 512), (512, T)), ((0, 512), (512, T)), ((0, 512), (512, T)), ((0, 256), (256, 512), (512, T)), ((0, 512), (512, T))]
-ON_SCALAR = [512,512,512,512,640,640]
+ON_SCALAR = [256,512,512,512,640,512]
 PLANES = 4
 
 
@@ -54,12 +53,11 @@ def tile_routed_moe_kernel(tc, xT, w_words, w_scales, gate, offs, out):
         s_rows = w_scales.bitcast(I32).rearrange("e a q n -> q (e a) n")
         s_tile = weight_planes[:].bitcast(I32).rearrange("p (s n) -> p s n", s=E * PASSES)
         for a in range(PASSES):
-            for lo, hi in LOADS[a]:
-                nc.sync.dma_start(out=raw[a][:, :, lo:hi], in_=x_rows[a][:, :, lo:hi])
+            nc.sync.dma_start(out=raw[a][:], in_=x_rows[a])
             if a == 0:
                 nc.sync.dma_start(offsets[:], offs)
-                for q in range(4):
-                    nc.sync.dma_start(out=s_tile[32 * q : 32 * q + 4], in_=s_rows[4 * q : 4 * q + 4])
+        for q in range(4):
+            nc.sync.dma_start(out=s_tile[32 * q : 32 * q + 4], in_=s_rows[4 * q : 4 * q + 4])
         for e in range(E):
             for lo, hi in ((0, PLANES), (PLANES, PASSES)):
                 nc.sync.dma_start(out=weights[e][:, lo:hi, :], in_=w_rows[e][:, lo:hi, :])
@@ -78,11 +76,8 @@ def tile_routed_moe_kernel(tc, xT, w_words, w_scales, gate, offs, out):
         for a in range(PASSES):
             g, j = a // PLANES, a % PLANES
             cut = ON_SCALAR[a]
-            for lo, hi in LOADS[a]:
-                if lo < cut:
-                    interleave(nc.scalar.copy, a, lo, min(hi, cut))
-                if hi > cut:
-                    interleave(nc.vector.tensor_copy, a, max(lo, cut), hi)
+            interleave(nc.scalar.copy, a, 0, cut)
+            interleave(nc.vector.tensor_copy, a, cut, T)
             for lo, hi in ((0, WIDE), (WIDE, T)):
                 nc.vector.quantize_mx(
                     out=words[a][:, lo:hi].bitcast(FP8X4),

from contextlib import ExitStack

import concourse.mybir as mybir

F32 = mybir.dt.float32
BF16 = mybir.dt.bfloat16
I32 = mybir.dt.int32
U32 = mybir.dt.uint32
U16 = mybir.dt.uint16
U8 = mybir.dt.uint8
FP8X4 = mybir.dt.float8_e4m3fn_x4
MULT = mybir.AluOpType.mult

K, T, E, C, N = 3072, 768, 2, 256, 384
P = 128
PASSES = K // 512
BLOCKS = N // P
SLOTS = E * C
FLOPS = 2 * K * N * SLOTS

WIDE = 512
ON_SCALAR = [256,512,512,512,640,512]
PLANES = 4


def tile_routed_moe_kernel(tc, xT, w_words, w_scales, gate, offs, out):
    nc = tc.nc
    with ExitStack() as ctx:
        held = ctx.enter_context(tc.tile_pool(name="held", bufs=1))
        psum = ctx.enter_context(tc.psum_pool(name="psum", bufs=1))

        offsets = held.tile([P, SLOTS // 16], U16, name="offsets")
        raw = [held.tile([P, 4, T], F32, name=f"raw{a}") for a in range(PASSES)]
        grouped = [held.tile([P, T, 4], BF16, name=f"grouped{a}", align_bytes=64) for a in range(PASSES)]
        words = [held.tile([P, T], U32, name=f"words{a}", align_bytes=64) for a in range(PASSES)]
        planes = [held.tile([P, T], U8, name=f"planes{g}", align_bytes=64) for g in range(2)]
        slot_words = [held.tile([P, SLOTS], U32, name=f"slot_words{a}", align_bytes=64) for a in range(PASSES)]
        slot_planes = [held.tile([P, SLOTS], U8, name=f"slot_planes{g}", align_bytes=64) for g in range(2)]
        weights = [held.tile([P, PASSES, N], I32, name=f"weights{e}", align_bytes=64) for e in range(E)]
        weight_planes = held.tile([P, E * PASSES * N], U8, name="weight_planes", align_bytes=64)
        gates = held.tile([P, SLOTS], F32, name="gates")
        windows = [held.tile([P, T], F32, name=f"window{b}") for b in range(BLOCKS)]
        scaled = [[held.tile([P, C], F32, name=f"scaled{b}_{e}") for e in range(E)] for b in range(BLOCKS)]

        nc.vector.memset(weight_planes[:].bitcast(I32), 0)
        for g in range(2):
            nc.gpsimd.memset(planes[g][:], 0)
        for b in range(BLOCKS):
            nc.gpsimd.memset(windows[b][:], 0.0)

        x_rows = xT.rearrange("(a p t) n -> a p t n", p=P, t=4)
        w_rows = w_words.rearrange("e a p n r -> e a p (n r)").bitcast(I32).rearrange("e a p n -> e p a n")
        s_rows = w_scales.bitcast(I32).rearrange("e a q n -> q (e a) n")
        s_tile = weight_planes[:].bitcast(I32).rearrange("p (s n) -> p s n", s=E * PASSES)
        for a in range(PASSES):
            nc.sync.dma_start(out=raw[a][:], in_=x_rows[a])
            if a == 0:
                nc.sync.dma_start(offsets[:], offs)
        for q in range(4):
            nc.sync.dma_start(out=s_tile[32 * q : 32 * q + 4], in_=s_rows[4 * q : 4 * q + 4])
        for e in range(E):
            for lo, hi in ((0, PLANES), (PLANES, PASSES)):
                nc.sync.dma_start(out=weights[e][:, lo:hi, :], in_=w_rows[e][:, lo:hi, :])
            if e == 0:
                nc.sync.dma_start(out=gates[:], in_=gate[0:P, :])

        def interleave(copy, a, lo, hi):
            copy(
                out=grouped[a][:, lo:hi, :].rearrange("p (c i) t -> p c t i", i=4),
                in_=raw[a][:, :, lo:hi].rearrange("p t (c i) -> p c t i", i=4),
            )

        def gather(dst, src, lo, hi):
            nc.vector.tensor_copy(out=dst[:, lo:hi], in_=src[:].indirect(offsets[:, lo // 16 : hi // 16]))

        for a in range(PASSES):
            g, j = a // PLANES, a % PLANES
            cut = ON_SCALAR[a]
            interleave(nc.scalar.copy, a, 0, cut)
            interleave(nc.vector.tensor_copy, a, cut, T)
            for lo, hi in ((0, WIDE), (WIDE, T)):
                nc.vector.quantize_mx(
                    out=words[a][:, lo:hi].bitcast(FP8X4),
                    scales=planes[g][4 * j : P, lo:hi],
                    in_=grouped[a][:, lo:hi, :].rearrange("p c t -> p (c t)"),
                )
            for lo, hi in ((0, C), (C, SLOTS)) if a == PASSES - 1 else ((0, SLOTS),):
                gather(slot_words[a], words[a], lo, hi)
                if a in (PLANES - 1, PASSES - 1):
                    gather(slot_planes[g], planes[g], lo, hi)

        def multiply(sums, e, b, a):
            g, j = a // PLANES, a % PLANES
            col = (e * PASSES + a) * N + b * P
            nc.tensor.matmul_mx(
                out=sums[b][:],
                lhsT=weights[e][:, a, b * P : (b + 1) * P].bitcast(FP8X4),
                lhsT_scale=weight_planes[:, col : col + P],
                rhs=slot_words[a][:, e * C : (e + 1) * C].bitcast(FP8X4),
                rhs_scale=slot_planes[g][4 * j : P, e * C : (e + 1) * C],
                start=(a == 0),
                stop=(a == PASSES - 1),
            )

        for e in range(E):
            sums = [psum.tile([P, C], F32, name=f"sums{b}") for b in range(BLOCKS)]
            if e == 0:
                for a in range(PLANES):
                    for b in range(BLOCKS):
                        multiply(sums, e, b, a)
            for b in range(BLOCKS):
                for a in range(PLANES if e == 0 else 0, PASSES):
                    multiply(sums, e, b, a)
                nc.scalar.copy(scaled[b][e][:], sums[b][:])
                nc.vector.tensor_tensor(
                    windows[b][:].indirect(offsets[:, e * C // 16 : (e + 1) * C // 16]),
                    scaled[b][e][:],
                    gates[:, e * C : (e + 1) * C],
                    MULT,
                )
                if e == E - 1:
                    nc.sync.dma_start(out=out[b * P : (b + 1) * P, :], in_=windows[b][:])
